import numpy as np, ml_dtypes
CORES = [78,86,94,102,110,118]
N = 6
BF = ml_dtypes.bfloat16
L, H, M, E, HO, RO, C, R, ST, QO = 4096, 2048, 128, 32, 3, 6, 16, 80, 341, 4096
def parts(rng):
    v = rng.integers(0, 256, (N, 8, 16, L)); m = np.argsort(rng.random((N, 8, H)), axis=-1) + H
    return v, m, rng.integers(0, 1024, (N, 8, 16, 1)), rng.integers(0, 2048, (N, 8, 16, E // 16)), rng.integers(780, 1081, (N, 8, 1))
def joined(rng, n):
    p = np.tile(np.arange(L), (N, 8, 1))
    for r in range(N):
        for g in range(8):
            o = rng.permutation(L); s = int(n[r, g]); p[r, g, o[:s]] = o[s:2 * s]; p[r, g, o[s:2 * s]] = o[:s]
    return p
def left(rng, n):
    p = np.tile(np.arange(L), (N, 8, 1))
    for r in range(N):
        for g in range(8):
            s = int(n[r, g]); a, b = rng.permutation(H)[s:], H + rng.permutation(H)[s:]; p[r, g, a] = b; p[r, g, b] = a
    return p
def shares(rng):
    return (rng.choice(np.array([0.0, 0.1, 0.25, 0.4, 0.475]), (N, 8)) * L).astype(np.int64)
def first_hop(v, w, k):
    u = np.add.reduce(w[:, None] * np.roll(v, 8, axis=0), axis=0) & (L - 1)
    return (((u * u) >> 5)[:, None] + u[:, None] * np.ascontiguousarray(k.T).reshape(1, -1)) & (L - 1)
def plant(rng, v, w, k, a, ok):
    pool = rng.integers(0, 256, (16, H)); src, to = [], []
    for j, cs in enumerate(first_hop(pool, w, k).tolist()):
        if len(to) == len(a): break
        for c in cs:
            if ok[c]:
                ok[c] = False; src.append(j); to.append(c); break
    x = pool[:, src]; v[:, a[:len(to)]] = x
    v[:, to] = np.clip(np.roll(x, 8, axis=0) + rng.integers(-2, 3, x.shape), 0, 255)
    return np.array(to, np.int64)
def pack(v, p, m, w, k, t):
    return {"rec": np.ascontiguousarray(v.reshape(N, 128, L)).astype(np.float32).astype(BF), "pr": p.astype(np.int32), "mt": m.astype(np.int32),
            "w": w.reshape(N, 128, 1).astype(np.int32), "kk": np.ascontiguousarray(k.reshape(N, 128, E // 16)).astype(np.int32), "th": t.astype(np.int32)}
def setup_inputs(rng):
    v, m, w, k, t = parts(rng)
    return pack(v, joined(rng, shares(rng)), m, w, k, t)
def setup_inputs_room(rng):
    v, m, w, k, t0 = parts(rng)
    n = rng.choice(np.array([0, 1, C - 1, C, R - 1, R, R + 1, M - 1, M, M + 1, H]), (N, 8))
    n[0] = R; n[0, 6:] = np.array([1, M - 1]); n[1] = np.array([R, R + 1, R - 1, R, C, M, M + 1, 0]); n[N - 1] = R; n[N - 1, 6:] = np.array([C - 1, H])
    n[2] = rng.choice(np.array([M, M + 1, 2 * M]), 8); n[2, :2] = np.array([M, M + 1])
    t = np.where(rng.random((N, 8, 1)) < 0.5, 0, t0); t[0, :6] = 0; t[1, :4] = 0; t[N - 1, :6] = 0; t[2] = t0[2]; t[1, 5] = t0[1, 5]
    p = left(rng, n); every = np.arange(L)
    for g in range(8):
        a = np.nonzero(p[2, g, :H] == every[:H])[0][:M]
        plant(rng, v[2, g], w[2, g, :, 0], k[2, g], a, ((every >= H) & (p[2, g] != every)).tolist())
    o = rng.permutation(H); a = o[:M // 2]; ok = np.zeros(L, bool); ok[o[M // 2:]] = True
    s = np.concatenate([a, plant(rng, v[1, 5], w[1, 5, :, 0], k[1, 5], a, ok.tolist())])
    rest = np.setdiff1d(every[:H], s); b = H + rng.permutation(H)[:len(rest)]
    p[1, 5] = every; p[1, 5, rest] = b; p[1, 5, b] = rest
    return pack(v, p, m, w, k, t)
def setup_inputs_ties(rng):
    v, m, w, k, t = parts(rng); v = 64 * rng.integers(0, 4, v.shape); t = 64 * rng.integers(10, 17, t.shape)
    v[:, 1::2] = v[:, 1::2][..., rng.integers(0, 64, L)]
    return pack(v, joined(rng, shares(rng)), m, w, k, t)
def setup_inputs_alike(rng):
    v, m, w, k, t = parts(rng); n = shares(rng); n[:, 0] = 0; p = joined(rng, n)
    w[:, 0] = 0; t[:, 0] = 1600
    for r in range(1, N):
        t[r, 0] = 4095; v[r, 0] = rng.integers(0, 40 if r % 2 == 0 else 120, (16, L))
        v[r, 0, :, 0] = 255; v[r, 0, :, 1] = 0
    v[1, 0, :, 1:] = 0
    k[:, 1] = k[:, 1, :1, :1]; t[:, 1] = 1200
    v[:, 2] = rng.integers(0, 256, (N, 1, 1)); v[::2, 2] = rng.integers(0, 256, (v[::2, 2].shape[0], 16, 1)); t[:, 2] = 1
    v[:, 3] = v[:, 3][..., rng.integers(0, 8, L)]
    m[:, 4] = H + np.arange(H); p[:, 4] = np.arange(L); o = rng.permutation(H)[:H // 2]; p[:, 4, o] = o + H; p[:, 4, o + H] = o
    for z in (v, m, w, k, t, p): z[:, 5] = z[:1, 5]
    k[:, 6] = 0; t[:, 6] = 1300
    for r in range(N):
        old = v[r, 6].copy(); c, j = np.unique(first_hop(old, w[r, 6, :, 0], k[r, 6])[:, 0], return_index=True); v[r, 6][:, c] = old[:, j]
    o = np.arange(20, H - 20); p[:, 7] = np.arange(L)
    for r in range(N):
        b = H + rng.permutation(H)[:H - 40]; p[r, 7, o] = b; p[r, 7, b] = o
    return pack(v, p, m, w, k, t)
def setup_inputs_ends(rng):
    v, m, w, k, t = parts(rng)
    v = np.where(rng.random((N, 8, 1, L)) < 0.5, rng.choice(np.array([0, 0, 1, 254, 255, 255]), v.shape), v)
    w[:, ::2] = rng.choice(np.array([1, 1022, 1023]), (N, 4, 16, 1)); k[:, 1::2] = rng.choice(np.array([0, 1, 2046, 2047]), (N, 4, 16, E // 16))
    t = rng.choice(np.array([1, 4080, 4081, 4094, 4095]), t.shape); t[0, 0] = 4095; t[N - 1, 1] = 4095
    v[:, 3, :, ::7] = 255; v[:, 3, :, 1::7] = 0
    v[:, 4] = rng.integers(240, 256, (N, 16, L)); v[:, 4, :, ::9] = 255; t[:, 4] = 4080
    w[:, 4] = rng.integers(1022, 1024, (N, 16, 1)); w[::2, 4] = 1023
    return pack(v, joined(rng, shares(rng)), m, w, k, t)
def setup_inputs_spread(rng):
    v, m, w, k, t = parts(rng)
    v = (rng.random((N, 8, 16, L)) * np.exp2(8 * rng.random((N, 8, 1, L)))).astype(np.int64); w = np.exp2(10 * rng.random(w.shape)).astype(np.int64)
    k = np.exp2(11 * rng.random(k.shape)).astype(np.int64); t = np.minimum(np.exp2(7 + 5 * rng.random(t.shape)).astype(np.int64), 4095)
    return pack(np.minimum(v, 255), joined(rng, shares(rng)), m, np.minimum(w, 1023), np.minimum(k, 2047), t)
def check_inputs(d):
    bad = []; v = np.asarray(d["rec"]).astype(np.float32)
    if not np.all((v >= 0) & (v <= 255) & (v == np.floor(v))): bad.append("rec: whole numbers from 0 to 255")
    for k, lo, hi in (("pr", 0, L - 1), ("mt", H, L - 1), ("w", 0, 1023), ("kk", 0, 2047), ("th", 0, 4095)):
        if np.min(d[k]) < lo or np.max(d[k]) > hi: bad.append("range of " + k)
    p = np.clip(np.asarray(d["pr"]).astype(np.int64), 0, L - 1)
    if not np.all(np.take_along_axis(p, p, -1) == np.arange(L)): bad.append("pr: a partner's partner is the leaf itself")
    if not np.all(np.sort(np.asarray(d["mt"]), axis=-1) == np.arange(H, L)): bad.append("mt: each leaf of the second half once")
    return bad
def reference(rec, pr, mt, w, kk, th):
    G = N * 8; g = np.arange(G)[:, None]; X = (np.arange(16) + 8) & 15
    q = np.ascontiguousarray(np.asarray(rec).astype(np.float32).astype(np.int32).reshape(G, 16, L).transpose(0, 2, 1))
    p = pr.astype(np.int64).reshape(G, L); first = mt.astype(np.int64).reshape(G, H)
    m = np.zeros((G, L), np.int64); m[:, :H] = first; m[g, first] = np.arange(H)
    wv = w.astype(np.int64).reshape(G, 1, 16); kv = np.ascontiguousarray(kk.astype(np.int64).reshape(G, 16, E // 16).transpose(0, 2, 1)).reshape(G, 1, E)
    t0 = th.astype(np.int64).reshape(G); J = np.repeat(t0[:, None], L, axis=1); lane = np.arange(M)
    for t in range(RO):
        order = (ST * t + np.arange(H)) & (H - 1)
        loose = (p[:, order] == order).astype(np.int64); place = np.add.accumulate(loose, axis=1) - 1
        gi, ci = np.nonzero((loose == 1) & (place < M))
        a = np.zeros((G, M), np.int64); live = np.zeros((G, M), bool); a[gi, place[gi, ci]] = order[ci]; live[gi, place[gi, ci]] = True
        A = q[g, a][:, :, X]; y = A; bd = np.full((G, M), 1 << 20); bc = np.zeros((G, M), np.int64)
        for h in range(HO):
            u = np.add.reduce(wv * y, axis=2) & (L - 1)
            c = (((u * u) >> 5)[:, :, None] + kv * u[:, :, None]) & (L - 1)
            D = np.add.reduce(np.abs(q[g[:, :, None], c] - A[:, :, None, :]), axis=3)
            D = np.where(c == a[:, :, None], 4095, D)
            e = np.argmin(D, axis=2)[:, :, None]
            D = np.take_along_axis(D, e, 2)[:, :, 0]; c = np.take_along_axis(c, e, 2)[:, :, 0]
            bc = np.where(D < bd, c, bc); bd = np.where(D < bd, D, bd)
            y = (A + q[g, m[g, p[g, c]]]) >> 1
        prop = live & (bd < J[g, bc]); key = M * bd + lane
        least = np.full((G, L), 1 << 30); gi, li = np.nonzero(prop)
        np.minimum.at(least, (gi, a[gi, li]), key[gi, li]); np.minimum.at(least, (gi, bc[gi, li]), key[gi, li])
        stand = prop & (least[g, a] == key) & (least[g, bc] == key)
        gi, li = np.nonzero(stand); sa, sc, sd = a[gi, li], bc[gi, li], bd[gi, li]
        old = p[gi, sc]; p[gi, old] = old; J[gi, old] = t0[gi]
        p[gi, sa] = sc; p[gi, sc] = sa; J[gi, sa] = sd; J[gi, sc] = sd
        va, vc = q[gi, sa], q[gi, sc]
        q[gi, sa] = va + np.clip(vc[:, X] - va, -1, 1); q[gi, sc] = vc + np.clip(va[:, X] - vc, -1, 1)
        no = live & (p[g, a] == a); place = np.add.accumulate(no.astype(np.int64), axis=1) - 1
        gi, li = np.nonzero(no & (place < R)); s = np.zeros((G, R), np.int64); has = np.zeros((G, R), bool)
        s[gi, place[gi, li]] = a[gi, li]; has[gi, place[gi, li]] = True
        v = q[g, s]; come = np.zeros_like(v); there = np.zeros_like(has); i = np.arange(G)
        for d in range(1, N):
            src = ((i // 8 - d) % N) * 8 + ((i - d) & 7); b = slice((d - 1) * C, d * C)
            come[:, b] = v[src, b]; there[:, b] = has[src, b]
        gi, k = np.nonzero(has & there); q[gi, s[gi, k]] = come[gi, k]
        gi, k = np.nonzero(has[:, 1::2]); x, z = s[gi, 2 * k], s[gi, 2 * k + 1]; mx, mz = m[gi, x], m[gi, z]
        m[gi, x] = mz; m[gi, z] = mx; m[gi, mx] = z; m[gi, mz] = x
        hx, hz, hmx, hmz = q[gi, x, 8:], q[gi, z, 8:], q[gi, mx, 8:], q[gi, mz, 8:]
        q[gi, x, 8:] = hz; q[gi, z, 8:] = hx; q[gi, mx, 8:] = hmz; q[gi, mz, 8:] = hmx
    yq = np.ascontiguousarray(q[:, :QO].transpose(0, 2, 1)).reshape(N, 128, QO)
    return {"yq": yq.astype(np.float32).astype(BF), "yp": p.reshape(N, 8, L).astype(np.float32), "ym": np.ascontiguousarray(m[:, :H]).reshape(N, 8, H).astype(np.float32)}

from concourse.bass import DstId, RemoteDMATransfer
from concourse.mybir import AluOpType as A, AxisListType, ActivationFunctionType as F

RO, ST, NR = 6, 341, 6
TW = 4496
f4, b2, i4, u2 = "float32", "bfloat16", "int32", "uint16"
_S = {}
for _n, _w, _d in [
        ("Q", TW, b2), ("PJ", TW, f4), ("M", TW, f4), ("IOTA", 4224, f4), ("DIG", 4096, b2), ("TMP", 4096, b2),
        ("LEAFV", 2048, f4), ("ROW", 2048, b2), ("SG", 2048, b2),
        ("PI", 8, i4), ("PC", 32, f4), ("JM", 128, f4), ("JR", 128, f4), ("J", 384, f4), ("BO", 128, b2), ("BOF", 128, f4),
        ("EQR", 128, f4), ("MK", 128, f4), ("MKB", 128, b2), ("SEG", 128, f4), ("ONE", 128, f4), ("ID2", 256, b2), ("IDP", 128, b2),
        ("XP", 128, b2), ("T1", 128, b2), ("ZM", 144, b2), ("ZG", 144, b2), ("TRI", 128, b2), ("KEYW", 128, b2), ("LC", 128, b2),
        ("COLB", 128, b2), ("CC", 96, f4), ("CU", 32, u2), ("WM", 512, b2), ("WB", 8, b2), ("K32", 32, f4), ("KD", 32, f4),
        ("INI", 16, i4), ("INF", 8, f4), ("G8", 128, f4), ("PRI", 256, i4), ("PRF", 256, f4), ("PRL", 256, f4), ("PRH", 512, b2),
        ("MTI", 128, i4), ("MTF", 128, f4), ("MTU", 128, u2), ("MTH", 256, b2),
        ("G0", 2048, b2), ("G1", 2048, b2), ("MX0", 2048, b2), ("MX1", 2048, b2), ("CW", 2048, i4), ("CI", 256, i4), ("CO", 256, u2),
        ("PEN", 256, b2), ("US", 128, f4), ("SI", 64, i4), ("SF", 64, f4), ("KI", 32, i4), ("SU", 64, u2),
        ("R1", 128, f4), ("C1", 128, f4), ("R2", 128, f4), ("C2", 128, f4), ("R3", 128, f4), ("C3", 128, f4), ("YS", 128, f4), ("Y2", 128, b2),
        ("QA", 144, b2), ("AW", 144, f4), ("AH", 128, f4), ("AB", 128, b2), ("AEX", 256, f4), ("SA", 128, f4), ("LV", 128, f4),
        ("AF", 16, f4), ("EF", 96, f4), ("EU", 32, u2), ("VAL", 24, f4), ("X2", 256, f4), ("TB", 3072, b2), ("DG", 128, b2), ("DFR", 256, f4),
        ("DIF", 128, f4), ("THT", 128, f4), ("QC", 128, b2), ("DC", 256, b2), ("NV", 256, b2), ("OF", 96, f4), ("OU", 32, u2),
        ("FL", 128, f4), ("CUM", 128, f4), ("JK", 1024, b2), ("ACC", 16, f4), ("SS", 80, b2), ("SB", 480, b2), ("LAND", 480, b2),
        ("MF", 64, f4), ("MU", 48, u2), ("RM", 160, f4), ("RM2", 160, f4), ("QM", 320, b2), ("MG", 400, b2),
        ("FW", 128, b2), ("CB", 128, f4), ("RK", 144, f4), ("LE", 128, b2), ("LF", 192, f4), ("LU", 16, u2), ("PV", 256, f4),
        ("KS", 256, f4), ("SEG2", 128, f4)]:
    _S[_n] = ("sbuf", [128, _w], _d)
BANKS = ["U0", "U1", "D0", "D1", "RA0", "RA1", "Y0", "Y1"]
for _n in BANKS:
    _S[_n] = ("psum", [128, 512], f4)
SCRATCH = _S
NDMA = 40
SEMAPHORES = ["v", "s", "t", "g", "sent"] + ["arr%d" % i for i in range(RO)] + ["d%d" % i for i in range(NDMA)]

CY, PE, GA, SC = 1.04, 0.52, 1.56, 3.8
WAKE = 130.0
ARR = 5000.0
LEAD = 2500.0
TOL = 0.0
GAP = 1000.0
CUTS = [0, 512, 1024, 1536, 1920, 2048]
NV = 4
SGV = 1536
BIG, SEGB = 2.0 ** 26, 2.0 ** 27
M0 = 1.5 * 2 ** 23
M2 = 1.5 * 2 ** 24
M32 = -2.0 ** 29 + 2.0 ** 17
WC = 2.0 ** 33


def V(n, a=0, b=None, s=1, p0=0, p1=128):
    return (n, a, SCRATCH[n][1][1] if b is None else b, s, p0, p1, None)


def IX(win, off):
    return win[:6] + (off,)


def _n(x):
    return 16 * (x[6][2] - x[6][1]) if x[6] else (x[2] - x[1] + x[3] - 1) // x[3]


def _isv(x):
    return isinstance(x, tuple)


def _two(x):
    return SCRATCH[x[0]][2] in (b2, u2)


def _meet(x, y):
    if x[1] >= y[2] or y[1] >= x[2] or x[4] >= y[5] or y[4] >= x[5]:
        return False
    return not (x[3] == y[3] and x[3] > 1 and (x[1] - y[1]) % x[3])


def build():
    ops = []
    lead = [0.0]

    def add(e, kind, out, ins, args, cost, hold=None, grp=None, extra=()):
        rd = [x for x in ins if _isv(x)]
        rd += [x[6] for x in rd + [out] if _isv(x) and x[6]]
        ops.append(dict(e=e, k=kind, out=out, ins=ins, a=args, c=cost, h=cost if hold is None else hold, g=grp, b=lead[0],
                        rd=rd, wr=[x for x in (out,) + tuple(extra) if _isv(x)]))

    def vc(out, ins, two=False, half=True):
        if out[6]:
            return 50 + _n(out) * SC * CY
        if ins[0][6]:
            return 50 + _n(out) * GA * CY
        k = 2.0 if two and all(x[0] not in BANKS for x in ins) else 1.0
        if half and all(_two(x) for x in [out] + ins):
            k *= 0.5
        return max(64, max(_n(x) for x in [out] + ins) * k) * CY

    def cp(o, i): add("v", "cp", o, [i], (), vc(o, [i]))
    def tt(o, a, b, op): add("v", "tt", o, [a, b], (op,), vc(o, [a, b], True))
    def ts(o, a, s1, op0, s2=None, op1=None): add("v", "ts", o, [a, s1, s2], (op0, op1), vc(o, [a]))
    def ms(o, c): add("v", "ms", o, [], (c,), vc(o, [o]))
    def red(o, i): add("v", "red", o, [i], (), vc(o, [i], half=False))
    def scan(o, a, b, op0, op1): add("v", "scan", o, [a, b], (op0, op1), vc(o, [a, b]))
    def pick(o, i): scan(o, V("SEG", 0, _n(i)), i, A.add, A.min)
    def after(x): ops[-1]["rd"].append(x)

    def act(o, i, f=F.Identity, bias=0.0, scale=1.0, acc=None):
        add("s", "act", o, [i, bias, scale], (f, acc), vc(o, [i], half=False) + (15 if i[6] else 0) + (20 if acc else 0), extra=(acc,))
    gid = [0]

    def mm(lst):
        gid[0] += 1
        for j, (o, l, r) in enumerate(lst):
            add("t", "mm", o, [l, r], (j == 0, j == len(lst) - 1), max(64, _n(r)) * PE * (1 if _two(l) else 4), grp=gid[0])

    def iota(o, pat, base=0, cm=0): add("g", "iota", o, [], (pat, base, cm), 130 + 2 * _n(o) * CY)
    nd = [0]

    def dma(e, o, i, nbytes, slow=False):
        add(e, "dma", o, [i], (nd[0], slow), 2000 + nbytes / 200.0, 80)
        nd[0] += 1
    col = lambda n, j: V(n, j, j + 1)
    cmpv = lambda n, a, k: V(n, a + 15, a + 16 * k, 16)

    lead[0] = 1e6
    dma("g", V("INI", 0, 1), "w", 512, True)
    dma("g", V("INI", 4, 5, 1, 0, 8), "th", 32, True)
    dma("y", V("PRI"), "pr", 131072)
    dma("s", V("MTI"), "mt", 65536)
    dma("s", V("INI", 2, 4), "kk", 1024)
    dma("y", V("Q", 0, 2048), "rec0", 524288)
    dma("y", V("Q", 2048, 4096), "rec1", 524288)
    lead[0] = 0.0
    iota(V("PI", 0, 1), [[0, 1]], 0, 1)
    iota(V("JR"), [[0, 8], [1, 16]])
    iota(V("JM"), [[1, 8], [0, 16]])
    iota(V("J"), [[1, 384]])
    iota(V("PRL"), [[1, 256]], 0, 256)
    iota(V("LEAFV"), [[1, 128], [128, 16]])
    iota(V("IOTA"), [[1, 4224]])
    iota(V("DIG"), [[1, 64], [0, 64]])
    iota(V("TMP"), [[0, 64], [1, 64]])
    for j, (sh, mk) in enumerate([(4, 7), (0, 15), (0, 1), (0, 3)]):
        ts(col("PI", 1 + j), col("PI", 0), sh, A.arith_shift_right, mk, A.bitwise_and)
    cp(V("PC", 0, 5), V("PI", 0, 5))
    pcol, gcol, rcol, par = [col("PC", j) for j in range(4)]
    hm, hn, r8, z15, ro, rx, nsg, kw, thf, g4k = [col("PC", j) for j in range(5, 15)]
    ts(hm, rcol, 8, A.is_ge)
    ts(hn, rcol, 8, A.is_lt)
    ts(col("PC", 16), hm, -16, A.mult, 8, A.add)
    tt(r8, col("PC", 16), rcol, A.add)
    ts(z15, gcol, 16, A.mult, 15, A.add)
    ts(nsg, par, 2, A.mult, -1, A.add)
    tt(rx, rcol, nsg, A.subtract)
    tt(ro, rx, par, A.add)
    ts(g4k, gcol, 4096, A.mult)
    ts(V("BO"), V("JM"), gcol, A.is_equal)
    ts(V("EQR"), V("JR"), rcol, A.is_equal)
    for r in range(16):
        ts(V("ROW", 128 * r, 128 * r + 128), V("BO"), col("EQR", r), A.mult)
    ts(V("PRL"), V("PRL"), g4k, A.subtract)
    tt(V("PRF"), V("PRI"), V("PRL"), A.subtract)
    cp(V("PRH", 0, 256), V("PRF"))
    tt(V("PRH", 256, 512), V("PRF"), V("PRH", 0, 256), A.subtract)
    ts(V("G8", 0, 128, 1, 0, 8), V("JM", 0, 128, 1, 0, 8), V("PC", 0, 1, 1, 0, 8), A.is_equal)
    cp(V("INF", 4, 5, 1, 0, 8), V("INI", 4, 5, 1, 0, 8))
    mm([(V("Y0", 0, 1), V("G8", 0, 128, 1, 0, 8), V("INF", 4, 5, 1, 0, 8))])
    ts(col("PC", 17), V("Y0", 0, 1), 4081, A.min, -2047, A.add)
    ts(thf, col("PC", 17), 1.0 / 4096, A.mult)
    for q in range(8):
        for j in range(2):
            o, l = V(BANKS[q], 256 * j, 256 * j + 256), V("ROW", 128 * (2 * q + j), 128 * (2 * q + j) + 128)
            mm([(o, l, V("PRH", 0, 256)), (o, l, V("PRH", 256, 512))])
        act(V("PJ", 512 * q, 512 * q + 512), V(BANKS[q]), bias=thf)
    ts(V("MTF"), V("MTI"), -2048, A.add)
    cp(V("MTU"), V("MTF"))
    cp(V("MTH", 0, 128), V("MTF"))
    tt(V("MTH", 128, 256), V("MTF"), V("MTH", 0, 128), A.subtract)
    ms(V("M", 2048, 4096), 0.0)
    for q in range(16):
        cp(IX(V("M", 2048, 4096), V("MTU", 8 * q, 8 * q + 8)), V("LEAFV", 128 * q, 128 * q + 128))
    for q in range(4):
        for j in range(4):
            o, l = V(BANKS[q], 128 * j, 128 * j + 128), V("ROW", 128 * (4 * q + j), 128 * (4 * q + j) + 128)
            mm([(o, l, V("MTH", 0, 128)), (o, l, V("MTH", 128, 256))])
        act(V("M", 512 * q, 512 * q + 512), V(BANKS[q]), bias=2048.0)
    ts(V("M", 4096, 4224), V("J", 0, 128), 4224, A.add)
    ts(V("M", 4224, TW), V("J", 0, TW - 4224), 4096, A.add)
    ms(V("PJ", 4096, TW), 0.75)
    ms(V("Q", 4096, TW), 0.0)
    cp(V("BOF"), V("BO"))
    ts(V("MK"), V("JR"), rcol, A.not_equal, BIG, A.mult)
    cp(V("MKB"), V("MK"))
    ts(V("SEG"), V("JR"), 0, A.is_equal, SEGB, A.mult)
    ms(V("ONE"), 1.0)
    ms(V("SEG2"), 0.0)
    ms(V("SEG2", 0, 128, 32), SEGB)
    ms(col("PC", 21), -2047.0)
    ident = V("ID2", 0, 128)
    ts(ident, V("J", 0, 128), pcol, A.is_equal)
    cp(V("ID2", 128, 256), ident)
    ts(V("IDP"), ident, 2.0 ** 22, A.mult)
    ts(V("T1"), V("JR"), r8, A.is_equal)
    tt(V("XP"), V("T1"), V("BO"), A.mult)
    ts(V("ZM"), V("J", 0, 144), z15, A.is_equal, 2048, A.mult)
    ts(V("ZG"), V("J", 0, 144), z15, A.is_equal, -1024, A.mult)
    ts(V("T1"), V("JR"), rcol, A.is_lt, -1, A.mult)
    tt(V("TRI"), V("T1"), V("BO"), A.mult)
    ts(col("PC", 18), col("EQR", 0), 2.0 ** 26, A.mult)
    ts(col("PC", 19), col("EQR", 8), 2.0 ** 20, A.mult, col("PC", 18), A.add)
    ts(kw, col("EQR", 15), 2.0 ** 13, A.mult, col("PC", 19), A.add)
    ts(V("KEYW"), V("BO"), kw, A.mult)
    ts(V("LC"), V("J", 0, 128), 64, A.add, col("EQR", 15), A.mult)
    cp(V("COLB"), V("J", 0, 128))
    j16 = lambda k: V("J", 0, 16 * k, 16)
    laneh, dump, ko, kx, lk = V("CC", 0, 8), V("CC", 8, 32), V("CC", 32, 37), V("CC", 40, 50), V("CC", 56, 64)
    ts(laneh, j16(8), rcol, A.add, 0.5, A.add)
    ts(dump, j16(24), rcol, A.add, 4096, A.add)
    ts(ko, j16(5), ro, A.add)
    ts(kx, j16(10), rx, A.add)
    ts(lk, laneh, 63.5, A.add, 2.0 ** 13, A.mult)
    cp(V("CU", 0, 10), kx)
    cp(V("CU", 16, 32), V("JM", 0, 128, 8))
    ts(col("INI", 8), col("INI", 0), 5, A.arith_shift_right)
    ts(col("INI", 9), col("INI", 0), 31, A.bitwise_and)
    ts(col("INF", 0), col("INI", 8), 16, A.mult)
    ts(col("INF", 1), col("INI", 9), 0.5, A.mult)
    ts(V("WB", 0, 2), V("INF", 0, 2), 2, A.mult)
    mm([(V("Y1", 0, 2), V("XP"), V("WB", 0, 2))])
    cp(V("INF", 5, 7), V("Y1", 0, 2))
    for j, c in enumerate([0, 1, 5, 6]):
        ts(V("WM", 128 * j, 128 * j + 128), V("BO"), col("INF", c), A.mult)
    cp(V("INF", 2, 4), V("INI", 2, 4))
    for e in range(2):
        ts(V("KD", 16 * e, 16 * e + 16), V("EQR", 0, 16), col("INF", 2 + e), A.mult, 32, A.mult)
    mm([(V("Y1", 0, 32), V("BOF"), V("KD"))])
    cp(V("K32"), V("Y1", 0, 32))
    ts(V("THT"), V("ONE"), thf, A.mult)
    ms(V("QA", 128, 144), -1024.0)
    ms(V("AW", 128, 144), 8192.0)
    ms(V("RK", 128, 144), 8192.0)
    for g in range(8):
        dma("y", V("DIG", 0, 4096, 1, 16 * g + 8, 16 * g + 16), V("TMP", 0, 4096, 1, 16 * g + 8, 16 * g + 16), 65536)
    Qw, PJw, Mw, IO = V("Q"), V("PJ"), V("M"), V("IOTA")
    af, aoff = V("AF", 0, 8), V("LU", 8, 16)

    def lanes(t):
        st = (ST * t) % 2048
        nth = col("PC", 20)
        if t == 0:
            ts(nth, thf, -1, A.mult)
        cuts = sorted(set([0, 512, 1024, 1536, SGV, 2048 - st, 2048]))
        for a, b in zip(cuts[:-1], cuts[1:]):
            s0 = (a + st) % 2048
            if a >= SGV:
                ts(V("SG", a, b), V("PJ", s0, s0 + b - a), thf, A.not_equal)
            else:
                act(V("SG", a, b), V("PJ", s0, s0 + b - a), F.Sign, bias=nth)
        for h in range(2):
            mm([(V("Y0", 64 * h, 64 * h + 64), V("ZG", 15 - r, 143 - r), V("SG", 1024 * h + r, 1024 * h + 1024, 16)) for r in range(16)])
        ts(V("FW"), V("Y0", 0, 128), 0, A.is_equal)
        mm([(V("Y0", 128, 256), V("BO"), V("FW"))])
        mm([(V("Y1", 0, 128), V("TRI"), V("FW"))])
        scan(V("CB"), V("ONE"), V("Y0", 128, 256), A.mult, A.add)
        tt(V("RK", 0, 128), V("CB"), V("Y1", 0, 128), A.add)
        for s in range(8):
            act(V("JK", 128 * s, 128 * s + 128), V("CB"), F.Sign, bias=col("CC", s), scale=-1.0, acc=col("ACC", s))
        acc = V("ACC", 0, 8)
        ts(V("LU", 0, 8), acc, 0.5, A.mult, 64, A.add)
        tt(V("LE"), IX(V("RK"), V("LU", 0, 8)), V("J", 0, 128), A.is_le)
        mm([(V("Y0", 0, 128), ident, V("MKB")), (V("Y0", 0, 128), V("BO"), V("LE"))])
        pick(V("LF", 0, 128), V("Y0", 0, 128))
        ts(V("LF", 128, 136), acc, 8, A.mult, 1024 + st, A.add)
        tt(V("SI", 16, 24), V("LF", 128, 136), cmpv("LF", 0, 8), A.add)
        ts(V("SI", 24, 32), V("SI", 16, 24), 2047, A.bitwise_and)
        cp(aoff, V("SI", 24, 32))
        cp(af, V("SI", 24, 32))
        ts(V("LF", 152, 160), acc, 128, A.is_ge, 65536, A.mult)
        ts(V("LV"), V("J", 0, 128), col("CB", 127), A.is_ge, -8192, A.mult)
        act(V("LV"), V("LV"), bias=thf)
        act(V("AW", 0, 128), IX(IO, aoff))
        act(V("X2", 128, 256), IX(IO, aoff))
        act(V("AEX"), IX(V("AF", 0, 8), V("CU", 16, 32)))
        for h in range(2):
            act(V("U%d" % h, 128, 256), V("AEX", 128 * h, 128 * h + 128))
        cp(V("VAL", 8, 16), af)
        ts(V("EF", 72, 80), af, -WC, A.mult)

    def choice(h, ki):
        a = 64 * h
        ts(V("SI", 32 + 4 * h, 36 + 4 * h), ki, 1023, A.bitwise_and)
        cp(V("SU", 4 * h, 4 * h + 4), V("SI", 32 + 4 * h, 36 + 4 * h))
        tt(V("R1", a, a + 64), IX(V("CW", 1024 * h, 1024 * h + 1024), V("SU", 4 * h, 4 * h + 4)), V("MK", 0, 64), A.add)
        pick(V("C1", a, a + 64), V("R1", a, a + 64))
        co = V("EU", 4 * h, 4 * h + 4)
        cp(co, cmpv("C1", a, 4))
        tt(V("R2", a, a + 64), IX(PJw, co), V("R1", a, a + 64), A.add)
        pick(V("C2", a, a + 64), V("R2", a, a + 64))

    def hop(k, h):
        a, s4, U, D, G, MX = 64 * h, 4 * h, "U%d" % h, "D%d" % h, "G%d" % h, "MX%d" % h
        src, w0 = (V("QA", a, a + 64), 256) if k == 0 else (V("Y2", a, a + 64), 0)
        mm([(V(U, 0, 64), ident, V("MKB", 0, 64)), (V(U, 0, 64), V("WM", w0, w0 + 128), src), (V(U, 0, 64), V("WM", w0 + 128, w0 + 256), src)])
        pick(V("US", a, a + 64), V(U, 0, 64))
        cp(V("SI", s4, s4 + 4), cmpv("US", a, 4))
        ts(V("SI", 8 + s4, 12 + s4), V("SI", s4, s4 + 4), 4095, A.bitwise_and)
        uf, sq, bi = V("SF", s4, s4 + 4), V("SF", 8 + s4, 12 + s4), V("SF", 16 + s4, 20 + s4)
        cp(uf, V("SI", 8 + s4, 12 + s4))
        tt(sq, V("SI", 8 + s4, 12 + s4), V("SI", 8 + s4, 12 + s4), A.mult)
        ts(bi, sq, -13, A.add, M32, A.add)
        b = 128 * h
        for s in range(4):
            ts(V("CI", b + 32 * s, b + 32 * s + 32), V("K32"), col("SF", s4 + s), A.mult, col("SF", 16 + s4 + s), A.add)
        c0 = 1024 * h + (128 * k - 256) % 1024
        cw = V("CW", c0, c0 + 128)
        ts(cw, V("CI", b, b + 128), 5, A.arith_shift_right, 4095, A.bitwise_and)
        cp(V("CO", b, b + 128), cw)
        tt(V("PEN", b, b + 128), cw, V(U, 128, 256), A.is_equal)
        for c0, c1 in zip(CUTS[:-1], CUTS[1:]):
            act(V(G, c0, c1), IX(Qw, V("CO", b + c0 // 16, b + c1 // 16)))
            for j in range(c0, c1, 128):
                tt(V(MX, j, j + 128), V(G, j, j + 128), V("RA%d" % h, j // 512 * 128, j // 512 * 128 + 128), A.max)
        for p in range(2):
            o, e0 = V(D, 64 * p, 64 * p + 64), 1024 * p
            mm([(o, ident, V("COLB", 64 * p, 64 * p + 64)), (o, V("IDP"), V("PEN", b + 64 * p, b + 64 * p + 64))]
               + [(o, V("ZG", 15 - r, 143 - r), V(G, e0 + r, e0 + 1024, 16)) for r in range(16)]
               + [(o, V("ZM", 15 - r, 143 - r), V(MX, e0 + r, e0 + 1024, 16)) for r in range(16)])
        scan(V("KS", b, b + 128), V("SEG2"), V(D, 0, 128), A.add, A.min)
        km = V("KS", b + 31, b + 128, 32)
        ki = V("KI", 8 * k + s4, 8 * k + s4 + 4)
        if k < 2:
            ts(ki, km, 128 * k - 256, A.add)
            choice(h, ki)
            ts(V("SU", 8 + s4, 12 + s4), cmpv("C2", a, 4), M0, A.add, -M0, A.add)
            tt(V("R3", a, a + 64), IX(Mw, V("SU", 8 + s4, 12 + s4)), V("MK", 0, 64), A.add)
            pick(V("C3", a, a + 64), V("R3", a, a + 64))
            cp(V("SU", 16 + s4, 20 + s4), cmpv("C3", a, 4))
            tt(V("YS", a, a + 64), IX(Qw, V("SU", 16 + s4, 20 + s4)), V("AH", a, a + 64), A.add)
            ts(V("Y2", a, a + 64), V("YS", a, a + 64), M2, A.add, -M2, A.add)
            if k == 1:
                tt(V("KI", 24 + s4, 28 + s4), V("KI", s4, s4 + 4), ki, A.min)
            return
        kb = V("KI", 24 + s4, 28 + s4)
        tt(kb, kb, km, A.min)
        choice(h, kb)
        e = lambda j: V("EF", 8 * j + s4, 8 * j + s4 + 4)
        pf, old = cmpv("C2", a, 4), V("VAL", s4, s4 + 4)
        ts(V("SI", 48 + s4, 52 + s4), kb, 256, A.add)
        ts(V("SI", 40 + s4, 44 + s4), V("SI", 48 + s4, 52 + s4), 10, A.arith_shift_right)
        tt(e(0), V("SI", 40 + s4, 44 + s4), V("EF", 80 + s4, 84 + s4), A.subtract)
        ts(e(1), e(0), -2047, A.add, 1.0 / 4096, A.mult)
        ts(old, pf, M0, A.add, -M0, A.add)
        ts(e(4), e(0), 1.0 / 8192, A.mult)
        tt(e(2), pf, e(1), A.subtract)
        tt(e(3), e(2), old, A.is_le)
        tt(e(5), e(3), e(4), A.max)
        ts(V("EU", 8 + s4, 12 + s4), e(5), 8192, A.mult, 4095, A.min)
        ts(e(6), e(5), 2.0 ** 33, A.mult)
        tt(e(7), e(6), V("CC", 56 + s4, 60 + s4), A.add)
        cp(V("VAL", 16 + s4, 20 + s4), cmpv("C1", a, 4))
        ts(e(8), cmpv("C1", a, 4), -WC, A.mult)
        act(V("X2", a, a + 64), IX(IO, V("EU", s4, s4 + 4)))
        tt(V("DIF", a, a + 64), V("X2", a, a + 64), V("X2", 128 + a, 192 + a), A.subtract)
        act(V("DFR", a, a + 64), V("DIF", a, a + 64), bias=col("PC", 21), scale=4096.0)
        act(V("DFR", 128 + a, 192 + a), V("DIF", a, a + 64), bias=col("PC", 21), scale=-4096.0)
        act(V("QC", a, a + 64), IX(Qw, V("EU", s4, s4 + 4)))
        tt(V("DC", a, a + 64), V("QC", a, a + 64), V("AB", a, a + 64), A.subtract)
        ts(V("DC", 128 + a, 192 + a), V("DC", a, a + 64), 1, A.min, -1, A.max)

    lanes(0)
    for t in range(RO):
        for h in range(2):
            a = 64 * h
            (act if h else cp)(V("QA", a, a + 64), IX(Qw, V("LU", 8 + 4 * h, 12 + 4 * h)))
            for j in range(32):
                mm([(V("RA%d" % h, 16 * j, 16 * j + 16), V("XP"), V("QA", a + j // 8 * 16, a + j // 8 * 16 + 16))])
        mm([(V("Y1", 0, 128), V("XP"), V("QA", 0, 128))])
        act(V("AH"), V("Y1", 0, 128), bias=-0.5)
        act(V("AB"), V("Y1", 0, 128))
        mm([(V("Y0", 0, 128), ident, V("MKB")), (V("Y0", 0, 128), V("BO"), V("QA", 0, 128))])
        pick(V("SA"), V("Y0", 0, 128))
        tt(V("EF", 80, 88), cmpv("SA", 0, 8), V("LF", 152, 160), A.subtract)
        for k in range(3):
            for h in range(2):
                lead[0] = LEAD * (1 - h)
                hop(k, h)
        lead[0] = 0.0
        doff = V("EU", 8, 16)
        tt(V("DG"), IX(V("DIG"), doff), V("LC"), A.max)
        for s in range(8):
            tb, bk = 384 * s, ("D0", "RA0", "U0", "Y0", "D1", "RA1", "U1")[s % 7]
            lead[0] = 300.0 * (8 - s)
            act(V("TB", tb, tb + 128), V("X2", 0, 128), F.Abs, bias=col("EF", 64 + s), scale=WC)
            act(V("TB", tb + 128, tb + 256), V("X2", 128, 256), F.Abs, bias=col("EF", 64 + s), scale=WC)
            for h in range(2):
                act(V("TB", tb + 256 + 64 * h, tb + 320 + 64 * h), V("X2", 64 * h, 64 * h + 64), F.Abs, bias=col("EF", 72 + s), scale=WC)
            mm([(V(bk, 0, 384), ident, V("TB", tb, tb + 384))]
               + [(V(bk, 128 * j, 128 * j + 128), V("KEYW"), V("DG")) for j in range(3)])
            if s < NV:
                red(col("EF", 88 + s), V(bk, 0, 384))
            else:
                act(V("JK", 384 * (s % 2), 384 * (s % 2) + 384), V(bk, 0, 384), F.Relu, bias=col("EF", 56 + s), scale=-1.0, acc=col("OF", s))
        lead[0] = 0.0
        tt(V("OF", 0, NV), V("EF", 56, 56 + NV), V("EF", 88, 88 + NV), A.subtract)
        for j in range(3):
            tt(V("OF", 24 + 8 * j, 32 + 8 * j), V("OF", 0, 8), V("VAL", 8 * j, 8 * j + 8), A.add)
        tt(V("OF", 48, 72), V("OF", 24, 48), dump, A.min)
        cp(V("OU", 0, 24), V("OF", 48, 72))
        ts(V("OF", 72, 80), V("OF", 0, 8), 0, A.is_equal, TW - 1, A.mult)
        tt(V("OF", 80, 88), V("OF", 72, 80), af, A.max)
        cp(V("OU", 24, 32), V("OF", 80, 88))
        mm([(V("Y1", 0, 128), V("XP"), V("DC", 128, 256))])
        tt(V("NV", 0, 128), V("QA", 0, 128), V("Y1", 0, 128), A.add)
        tt(V("NV", 128, 256), V("QC"), V("DC", 128, 256), A.subtract)
        tt(V("PV", 128, 256), IX(IO, doff), V("DFR", 128, 256), A.add)
        tt(V("PV", 0, 128), IX(IO, doff), V("DFR", 0, 128), A.add)
        join = lambda j: ts(IX(PJw, V("OU", 8 + 8 * j, 16 + 8 * j)), V("PV", 128 * j, 128 * j + 128), 1.0 / 4096, A.mult, 0.0, A.add)
        join(1)
        tt(V("FL"), IX(PJw, V("OU", 24, 32)), V("LV"), A.is_equal)
        scan(V("CUM"), V("ONE"), V("FL"), A.mult, A.add)
        cp(IX(PJw, V("OU", 0, 8)), V("THT"))
        after(V("CUM"))
        for s in range(5):
            act(V("JK", 128 * s, 128 * s + 128), V("CUM"), F.Sign, bias=col("CC", s), scale=-1.0, acc=col("ACC", 8 + s))
        lam = V("MU", 0, 5)
        ts(lam, V("ACC", 8, 13), 0.5, A.mult, 64, A.add)
        cp(V("SS"), IX(V("QA"), lam))
        for d in range(1, NR):
            mm([(V("U0", 16 * d - 16, 16 * d), V("ID2", 128 - 16 * d, 256 - 16 * d), V("SS", 16 * d - 16, 16 * d))])
        sb, land = V("SB", 80 * t, 80 * t + 80), V("LAND", 80 * t, 80 * t + 80)
        cp(sb, V("U0", 0, 80))
        add("g", "send", None, [sb], (t,), 1000)
        add("x", "arrive", land, [sb], (t,), ARR, 0)
        join(0)
        join(1)
        cp(IX(Qw, V("OU", 8, 24)), V("NV"))
        after(sb)
        nref = col("CUM", 127)
        tt(V("R1", 0, 80), IX(V("AW"), lam), V("MK", 0, 80), A.add)
        pick(V("C1", 0, 80), V("R1", 0, 80))
        tt(V("MF", 0, 5), cmpv("C1", 0, 5), V("CC", 8, 13), A.min)
        cp(V("MU", 6, 11), V("MF", 0, 5))
        ts(V("MF", 8, 13), ko, nref, A.is_ge, 8192, A.mult)
        tt(V("MF", 16, 21), V("MF", 8, 13), V("MF", 0, 5), A.add)
        tt(V("MF", 24, 29), V("MF", 16, 21), V("CC", 8, 13), A.min)
        s2 = V("MU", 12, 17)
        cp(s2, V("MF", 24, 29))
        cp(V("MU", 23, 28), V("MF", 24, 29))
        ts(V("MF", 32, 37), ko, nref, A.is_ge, nsg, A.mult)
        tt(V("MF", 40, 45), V("MF", 32, 37), V("CC", 40, 45), A.add)
        cp(V("MU", 30, 35), V("MF", 40, 45))
        tt(V("R3", 0, 80), IX(Mw, s2), V("MK", 0, 80), A.add)
        pick(V("C3", 0, 80), V("R3", 0, 80))
        m2 = V("MU", 18, 23)
        cp(m2, cmpv("C3", 0, 5))
        act(V("RM", 0, 80), IX(IO, s2))
        act(V("RM", 80, 160), IX(Mw, s2))
        act(V("RM2"), IX(V("RM"), V("CU", 0, 10)))
        cp(IX(Mw, V("MU", 18, 28)), V("RM2"))
        act(V("QM", 0, 80), IX(Qw, m2))
        act(V("QM", 80, 160), IX(V("QM", 0, 80), V("CU", 0, 5)), scale=hm)
        ts(V("QM", 160, 240), V("QM", 0, 80), hn, A.mult)
        tt(IX(Qw, m2), V("QM", 80, 160), V("QM", 160, 240), A.add)
        if t + 1 < RO:
            lanes(t + 1)
        else:
            for g in range(8):
                dma("y", V("PRF", 0, 256, 1, 16 * g, 16 * g + 16), V("PJ", 0, 4096, 1, 16 * g, 16 * g + 1), 16384)
            ts(V("PRF"), V("PRF"), M0, A.add, -M0, A.add)
            tt(V("PRF"), V("PRF"), V("PRL"), A.add)
            dma("s", "yp", V("PRF"), 131072)
            for g in range(8):
                dma("y", "ym%d" % g, V("M", 0, 2048, 1, 16 * g, 16 * g + 1), 8192)
            for j in range(2):
                act(V("TMP", 1024 * j, 1024 * j + 1024), V("Q", 2048 + 1024 * j, 3072 + 1024 * j))
            dma("s", "yq1", V("TMP", 0, 2048), 524288)
        act(V("MG", 0, 80), land, F.Abs)
        tt(V("MG", 80, 160), V("SS"), land, A.max)
        tt(V("MG", 160, 240), V("MG", 80, 160), V("MG", 0, 80), A.min)
        act(V("MG", 240, 320), IX(V("MG", 160, 240), V("MU", 30, 35)), scale=hm)
        ts(V("MG", 320, 400), V("MG", 160, 240), hn, A.mult)
        tt(IX(Qw, V("MU", 6, 11)), V("MG", 240, 320), V("MG", 320, 400), A.add)
    dma("y", "yq0", V("Q", 0, 1024), 262144)
    dma("s", "yq2", V("Q", 1024, 2048), 262144)
    assert nd[0] <= NDMA
    return ops


def _free(x, y):
    return x["e"] == "t" and y["e"] == "t" and (x["g"] == y["g"] or not _meet(x["out"], y["out"]))


def schedule(ops):
    last = {}
    for i, o in enumerate(ops):
        dep = set()
        acc = [(x, False) for x in o["rd"]] + [(x, True) for x in o["wr"]]
        for x, w in acc:
            for j, y, wy in last.get(x[0], ()):
                if x[0] in BANKS:
                    if w or wy or ops[j]["e"] != o["e"]:
                        dep.add(j)
                elif (w or wy) and _meet(x, y):
                    dep.add(j)
        for x, w in acc:
            l = last.setdefault(x[0], [])
            if w:
                if x[0] in BANKS:
                    l[:] = [z for z in l if o["e"] == "t" and z[2] and ops[z[0]]["e"] == "t" and not _meet(x, z[1])][-40:]
                elif x[3] == 1:
                    l[:] = [z for z in l if not (x[1] <= z[1][1] and z[1][2] <= x[2] and x[4] <= z[1][4] and z[1][5] <= x[5])]
            l.append((i, x, w))
        dep.discard(i)
        o["dep"] = dep
    n = len(ops)
    succ = [[] for _ in range(n)]
    for i, o in enumerate(ops):
        for j in o["dep"]:
            succ[j].append(i)
    same = lambda i, j: _free(ops[i], ops[j])
    lag = lambda j, i: 0.0 if same(i, j) else WAKE
    pr = [0.0] * n
    for i in range(n - 1, -1, -1):
        pr[i] = ops[i]["c"] + max([pr[k] + lag(i, k) for k in succ[i]] + [0.0])
    left = [len(o["dep"]) for o in ops]
    rdy = [0.0] * n
    cand = {e: [] for e in "vstgyx"}
    for i in range(n):
        if not left[i]:
            cand[ops[i]["e"]].append(i)
    free = {e: 0.0 for e in cand}
    order = {e: [] for e in cand}
    end = 0.0
    rank = lambda k: (pr[k] + ops[k]["b"], -k)
    for _ in range(n):
        best = None
        for e, l in cand.items():
            if l:
                t0 = max(free[e], min(rdy[i] for i in l))
                if best is None or t0 < best[0]:
                    best = (t0, e)
        t0, e = best
        i = max((k for k in cand[e] if rdy[k] <= t0 + 40.0), key=rank)
        top = max((k for k in cand[e] if rdy[k] < t0 + ops[i]["h"] - TOL or k == i), key=rank)
        if rank(top)[0] > rank(i)[0] + GAP:
            fit = [k for k in cand[e] if max(t0, rdy[k]) + ops[k]["h"] <= rdy[top] + TOL]
            i = max(fit, key=rank) if fit else top
        cand[e].remove(i)
        s = max(t0, rdy[i])
        free[e] = s + ops[i]["h"]
        ops[i]["at"] = s
        order[e].append(i)
        end = max(end, s + ops[i]["c"])
        for k in succ[i]:
            rdy[k] = max(rdy[k], s + ops[i]["c"] + lag(i, k))
            left[k] -= 1
            if not left[k]:
                cand[ops[k]["e"]].append(k)
    need = set(j for i, o in enumerate(ops) for j in o["dep"] if not same(i, j) and o["k"] != "arrive")
    cnt = {e: 0 for e in cand}
    for e, l in order.items():
        for i in l:
            o = ops[i]
            if o["k"] == "dma":
                o["sig"] = ("d%d" % o["a"][0], 16)
            elif o["k"] == "arrive":
                o["sig"] = ("arr%d" % o["a"][0], None)
            elif o["k"] != "send" and i in need:
                cnt[e] += 1
                o["sig"] = (e, cnt[e])
            else:
                o["sig"] = None
    return order, cnt, end


_PLAN = []


def rank_program(g, core, T, topo):
    rank = T.rank_of(core)
    if rank is None:
        return
    if not _PLAN:
        ops = build()
        _PLAN.append((ops, schedule(ops)))
    ops, (order, cnt, _) = _PLAN[0]
    N = len(T.cores)
    ext = {"w": T.w[:], "th": T.th[:], "pr": T.pr[:], "mt": T.mt[:], "kk": T.kk[:], "rec0": T.rec[:, 0:2048], "rec1": T.rec[:, 2048:4096],
           "yp": T.yp[:], "yq0": T.yq[:, 0:1024], "yq2": T.yq[:, 1024:2048], "yq1": T.yq[:, 2048:4096]}
    for k in range(8):
        ext["ym%d" % k] = T.ym[k:k + 1, :]

    def ap(x):
        if isinstance(x, str):
            return ext[x]
        if not _isv(x):
            return x
        a = T[x[0]][x[4]:x[5], x[1]:x[2]] if x[3] == 1 else T[x[0]][x[4]:x[5], x[1]:x[2]:x[3]]
        return a.indirect(ap(x[6])) if x[6] else a

    def deal(src):
        eng = None
        for d in range(1, N):
            e = topo.engines(src, T.cores[(T.rank_of(src) + d) % N])
            eng = e if eng is None else [x for x in eng if x in e]
        per = len(eng) // (N - 2)
        first = [(d, eng[per * (d - 1):per * d]) for d in range(1, N - 1)]
        return [first, [(N - 1, eng)]]
    arrive = sum(len(e) for d in range(1, N) for call in deal(T.cores[(rank - d) % N]) for dd, e in call if dd == d)
    sent = RO * sum(len(e) for call in deal(core) for _, e in call)
    qs = {"v": g.vector, "s": g.scalar, "t": g.tensor, "g": g, "y": g.sync}
    for e, q in qs.items():
        seen = {}
        for i in order[e]:
            o = ops[i]
            want = {}
            for j in o["dep"]:
                sg = ops[j]["sig"]
                if sg is None or _free(o, ops[j]):
                    continue
                want[sg[0]] = max(want.get(sg[0], 0), arrive if sg[1] is None else sg[1])
            for s, c in sorted(want.items()):
                if seen.get(s, 0) < c:
                    q.wait_ge(T.sem[s], c)
                    seen[s] = c
            k, a, out, ins = o["k"], o["a"], ap(o["out"]), [ap(x) for x in o["ins"]]
            if k == "send":
                for call in deal(core):
                    trs = []
                    for d, eng in call:
                        rid, pid, _ = topo.addr(T.cores[(rank + d) % N])
                        c0 = 80 * a[0] + 16 * (d - 1)
                        trs.append(RemoteDMATransfer(dst_ids=[DstId(rid=rid, pnc=pid)], dma_engine_mask=sum(1 << x for x in eng),
                                                     remote_sem=T.sem["arr%d" % a[0]], src=T.SB[:, c0:c0 + 16], dst=T.LAND[:, c0:c0 + 16]))
                    g.remote_dma_fused(trs, local_sem=T.sem["sent"])
                continue
            if k == "cp":
                r = q.tensor_copy(out, ins[0])
            elif k == "tt":
                r = q.tensor_tensor(out, ins[0], ins[1], a[0])
            elif k == "ts":
                r = q.tensor_scalar(out, ins[0], ins[1], ins[2], a[0], a[1]) if a[1] is not None else q.tensor_scalar(out, ins[0], ins[1], None, a[0])
            elif k == "ms":
                r = q.memset(out, a[0])
            elif k == "red":
                r = q.tensor_reduce(out, ins[0], AxisListType.X, A.min)
            elif k == "scan":
                r = q.tensor_tensor_scan(out, ins[0], ins[1], 0.0, a[0], a[1])
            elif k == "act":
                r = q.activation(out, ins[0], a[0], bias=ins[1], scale=ins[2], accum_out=ap(a[1]))
            elif k == "mm":
                r = q.matmul(out, ins[0], ins[1], a[0], a[1])
            elif k == "iota":
                r = q.iota(out, a[0], a[1], a[2], allow_small_or_imprecise_dtypes=True) if SCRATCH[o["out"][0]][2] != i4 else q.iota(out, a[0], a[1], a[2])
            else:
                r = q.dma_start(out, ins[0], allow_slow_non_contiguous=True) if a[1] else q.dma_start(out, ins[0])
            if o["sig"]:
                r.then_inc(T.sem[o["sig"][0]], 16 if k == "dma" else 1)
    for e in "vstg":
        if cnt[e]:
            g.wait_ge(T.sem[e], cnt[e])
    for o in ops:
        if o["k"] == "dma":
            g.wait_ge(T.sem[o["sig"][0]], 16)
    g.wait_ge(T.sem["sent"], sent)
